import numpy as np
CORES = [211,219,227,235,243,251,83,91,99,107,115,123]
N = 12
B, S = 16, 128
CAPP = 4
def entries(a): return a.T.reshape(-1)
def pack(v, P): return np.ascontiguousarray(np.asarray(v, np.int32).reshape(-1, P).T)
def lists(rng, how):
    Q = rng.integers(0, N * B, N * B)
    O = np.stack([rng.permutation(np.repeat(rng.permutation(N)[:B // CAPP], CAPP)) if how == "full" else rng.permutation(np.repeat(np.arange(N), CAPP))[:B] for r in range(N)])
    Q = (B * O + Q.reshape(N, B) % B).reshape(-1)
    if how == "alike": Q = (B * O + rng.integers(B)).reshape(-1)
    if how == "edge": Q = (B * O + np.where(rng.random((N, B)) < 0.5, 0, B - 1)).reshape(-1)
    if how == "full": Q = (B * O + (rng.integers(B) + np.stack([np.array([np.sum(O[r, :i] == O[r, i]) for i in range(B)]) for r in range(N)])) % B).reshape(-1)
    if how == "sorted": Q = np.sort(Q.reshape(N, B), axis=1).reshape(-1)
    return {"parent": np.broadcast_to(pack(Q, 16), (N, 16, N * B // 16)).copy()}
def setup_inputs(rng):
    return dict({"c": rng.standard_normal((N, 128, B * S), dtype=np.float32)}, **lists(rng, "uniform"))
def setup_inputs_alike(rng):
    d = setup_inputs(rng); d.update(lists(rng, "alike"))
    for k in ("c",): d[k] = (d[k].astype(np.float32) * 1048576.0).astype(d[k].dtype)
    return d
def setup_inputs_edge(rng):
    d = setup_inputs(rng); d.update(lists(rng, "edge"))
    for k in ("c",): d[k] = (d[k].astype(np.float32) * (1 / 1024.0)).astype(d[k].dtype)
    return d
def setup_inputs_full(rng):
    d = setup_inputs(rng); d.update(lists(rng, "full"))
    return d
def setup_inputs_sorted(rng):
    d = setup_inputs(rng); d.update(lists(rng, "sorted"))
    return d
def check_inputs(x):
    bad = []
    if x["parent"].min() < 0 or x["parent"].max() >= N * B: bad.append("parent out of range")
    if not all(np.array_equal(a, x["parent"][0]) for a in x["parent"]): bad.append("parent isn't alike on all ranks")
    if max(int(np.bincount(q // B, minlength=N).max()) for q in entries(x["parent"][0]).reshape(N, B)) > CAPP: bad.append("more than CAPP beams of a rank have their parents on one rank")
    return bad
def reference(c, parent):
    A = np.concatenate(list(c), axis=1).reshape(128, N * B, S)
    Y = A[:, entries(parent[0]), :]
    return {"y": np.stack([Y[:, B * r:B * r + B].reshape(128, B * S) for r in range(N)])}

@@ -1,0 +1,291 @@
+from concourse.bass import DstId, RemoteDMATransfer
+from concourse.mybir import AluOpType, ActivationFunctionType
+
+N, B, S, CAPP = 12, 16, 128, 4
+H = 4
+W = S // H
+SLOT = CAPP * W
+SL = B * W
+NCH = 4
+BCH = B // NCH
+NCORES = 256
+
+SCRATCH = {
+    "par": ("sbuf", [128, N], "int32"),
+    "cbuf": ("sbuf", [128, B, S], "float32"),
+    "slb": ("sbuf", [128, H * SL], "float32"),
+    "sendbuf": ("sbuf", [128, N * SLOT], "float32"),
+    "land": ("sbuf", [128, N * H * SLOT], "float32"),
+    "ybuf": ("sbuf", [128, B * S], "float32"),
+    "offS": ("sbuf", [128, N * CAPP * 2], "uint16"),
+    "offR": ("sbuf", [128, B * 8], "uint16"),
+    "ones": ("sbuf", [128, 128], "float32"),
+    "c32": ("sbuf", [128, 128], "float32"),
+    "c512": ("sbuf", [128, 128], "float32"),
+    "U": ("sbuf", [128, 16], "float32"),
+    "Irep": ("sbuf", [128, 128], "float32"),
+    "Kc": ("sbuf", [128, 48], "float32"),
+    "RcA": ("sbuf", [128, 48], "float32"),
+    "U8": ("sbuf", [128, 128], "float32"),
+    "I8": ("sbuf", [128, 128], "float32"),
+    "RcB": ("sbuf", [128, 128], "float32"),
+    "a4": ("sbuf", [128, 48], "int32"),
+    "src4": ("sbuf", [128, 48], "int32"),
+    "b4": ("sbuf", [128, 48], "int32"),
+    "M4": ("sbuf", [128, 48], "float32"),
+    "Mb4": ("sbuf", [128, 48], "float32"),
+    "E4": ("sbuf", [128, 48], "float32"),
+    "V4": ("sbuf", [128, 48], "float32"),
+    "colf": ("sbuf", [128, 4], "float32"),
+    "Dg8": ("sbuf", [128, 128], "float32"),
+    "Eq": ("sbuf", [128, 128], "float32"),
+    "EqU": ("sbuf", [128, 128], "float32"),
+    "ps1": ("psum", [128, 512], "float32"),
+    "ps2": ("psum", [128, 512], "float32"),
+    "ps3": ("psum", [128, 512], "float32"),
+    "ps4": ("psum", [128, 512], "float32"),
+}
+NEV = 48
+SEMAPHORES = ["parS", "winS", "arr", "lsem"] + ["e%d" % i for i in range(NEV)]
+
+
+def bits(mask):
+    return [e for e in range(16) if (mask >> e) & 1]
+
+
+def to_mask(engines):
+    m = 0
+    for e in engines:
+        m |= 1 << e
+    return m
+
+
+def common_mask(topo, src, dsts):
+    m = topo.mask(src, dsts[0])
+    for d in dsts[1:]:
+        m &= topo.mask(src, d)
+    return m
+
+
+def chip_workers(rc, T, topo):
+    same = [c for c in range(NCORES) if topo.host(c) == topo.host(rc) and topo.chip(c) == topo.chip(rc)]
+    ok = [c for c in same if c != rc and all(topo.may_write(c, d) for d in T.cores)]
+    return [rc] + ok[:H - 1]
+
+
+def calls_of(s, w, T, topo):
+    u0 = s // 2
+    units = [(u0 + 1 + t) % (N // 2) for t in range(N // 2)]
+    calls = []
+    for c in range(3):
+        ds = []
+        for u in units[2 * c:2 * c + 2]:
+            ds += [2 * u, 2 * u + 1]
+        ds = [d for d in ds if T.cores[d] != w]
+        eng = bits(common_mask(topo, w, [T.cores[d] for d in ds]))
+        q = len(eng) // 4
+        sizes = [q] * 4 if len(ds) == 4 else [2 * q, q, q]
+        call, at = [], 0
+        for d, n in zip(ds, sizes):
+            call.append((d, to_mask(eng[at:at + n]), n))
+            at += n
+        calls.append(call)
+    return calls
+
+
+def rank_program(g, core, T, topo):
+    V, Sc, Te, Sy = g.vector, g.scalar, g.tensor, g.sync
+    A = AluOpType
+    COPY = ActivationFunctionType.Copy
+    s, h, workers = None, None, None
+    for r, rc in enumerate(T.cores):
+        ws = chip_workers(rc, T, topo)
+        if core in ws:
+            s, h, workers = r, ws.index(core), ws
+    if s is None:
+        return
+    is_rank = h == 0
+    nev = [0]
+
+    def ev():
+        nev[0] += 1
+        return T.sem["e%d" % (nev[0] - 1)]
+
+    lsent = 0
+    P = slice(0, 16)
+
+    e_pm, e_parL = ev(), ev()
+    if is_rank:
+        V.memset(T.par[:, :], 0).then_inc(e_pm, 1)
+    e_ones, n_ones = ev(), 2
+    V.memset(T.ones[P, :], 1.0).then_inc(e_ones, 1)
+    V.memset(T.c32[P, :], float(W)).then_inc(e_ones, 1)
+    if is_rank:
+        V.memset(T.c512[P, :], float(H * SLOT)).then_inc(e_ones, 1)
+        n_ones = 3
+
+    e_ld = [ev() for _ in range(NCH)]
+    if is_rank:
+        Sy.wait_ge(e_pm, 1)
+        Sy.dma_start(T.par[P, :], T.parent[:, :]).then_inc(e_parL, 16)
+        for j in range(NCH):
+            q = Sc if j % 2 == 0 else Sy
+            q.dma_start(T.cbuf[:, BCH * j:BCH * (j + 1), :], T.c[:, BCH * S * j:BCH * S * (j + 1)]).then_inc(e_ld[j], 16)
+
+    e_c = ev()
+    g.wait_ge(e_ones, n_ones)
+    g.affine_select(T.U[P, 0:16], T.ones[P, 0:16], [[1, 16]], A.is_gt, 0.0, 0, -1).then_inc(e_c, 1)
+    g.affine_select(T.Irep[P, :], T.ones[P, :], [[0, 8], [1, 16]], A.is_equal, 0.0, 0, -1).then_inc(e_c, 1)
+    g.iota(T.Kc[P, :], [[0, N], [1, CAPP]], 0, 0, allow_small_or_imprecise_dtypes=True).then_inc(e_c, 1)
+    g.iota(T.RcA[P, :], [[0, 48]], 0, 1, allow_small_or_imprecise_dtypes=True).then_inc(e_c, 1)
+
+    e_cb = ev()
+    if is_rank:
+        g.wait_ge(e_parL, 16)
+        m = common_mask(topo, core, workers[1:])
+        ids = []
+        for w in workers[1:]:
+            rid, pid = topo.addr(w, core)
+            ids.append(DstId(rid=rid, pnc=pid))
+        g.remote_dma_fused([RemoteDMATransfer(dst_ids=ids, dma_engine_mask=m, remote_sem=T.sem.parS,
+                                              srcs=[T.par[:, :]], dsts=[T.par[:, :] for _ in ids], alu_op=0)],
+                           local_sem=T.sem.lsem)
+        lsent += len(bits(m))
+        V.wait_ge(e_parL, 16)
+        g.affine_select(T.U8[P, :], T.ones[P, :], [[1, 16], [0, 8]], A.is_gt, 0.0, 0, -1).then_inc(e_cb, 1)
+        g.affine_select(T.I8[P, :], T.ones[P, :], [[1, 16], [0, 8]], A.is_equal, 0.0, 0, -1).then_inc(e_cb, 1)
+        g.iota(T.RcB[P, :], [[0, 16], [SLOT, H], [16, 2]], 0, 1, allow_small_or_imprecise_dtypes=True).then_inc(e_cb, 1)
+    else:
+        V.wait_ge(T.sem.parS, len(bits(common_mask(topo, workers[0], workers[1:]))))
+
+    e1, e2, e3, e4, e5, e6, e7, e8 = [ev() for _ in range(8)]
+    Te.wait_ge(e_ones, n_ones)
+    Te.wait_ge(e_c, 4)
+    Te.matmul(T.ps2[:, 0:48], T.Irep[P, :], T.RcA[P, :], True, False)
+    for k in range(CAPP):
+        V.tensor_copy(T.a4[P, k:48:CAPP], T.par[P, :]).then_inc(e1, 1)
+    V.wait_ge(e1, CAPP)
+    V.tensor_scalar(T.src4[P, :], T.a4[P, :], 4, None, A.arith_shift_right).then_inc(e2, 1)
+    V.tensor_scalar(T.b4[P, :], T.a4[P, :], 15, None, A.bitwise_and).then_inc(e2, 1)
+    V.wait_ge(e2, 2)
+    V.tensor_scalar(T.M4[P, :], T.src4[P, :], float(s), None, A.is_equal).then_inc(e3, 1)
+    V.wait_ge(e3, 1)
+    Te.wait_ge(e3, 1)
+    Te.matmul(T.ps1[P, 0:48], T.U[P, 0:16], T.M4[P, :], True, True).then_inc(e4, 1)
+    V.tensor_tensor(T.Mb4[P, :], T.M4[P, :], T.b4[P, :], A.mult).then_inc(e5, 1)
+    V.wait_ge(e_c, 4)
+    V.wait_ge(e4, 1)
+    V.tensor_tensor(T.E4[P, :], T.ps1[P, 0:48], T.Kc[P, :], A.is_equal).then_inc(e5, 1)
+    V.wait_ge(e5, 2)
+    V.tensor_tensor(T.V4[P, :], T.E4[P, :], T.Mb4[P, :], A.mult).then_inc(e6, 1)
+    Te.wait_ge(e6, 1)
+    Te.matmul(T.ps2[:, 0:48], T.c32[P, :], T.V4[P, :], False, True).then_inc(e7, 1)
+    V.wait_ge(e7, 1)
+    for xh in range(2):
+        V.tensor_scalar(T.offS[:, xh:96:2], T.ps2[:, 0:48], float(16 * xh), None, A.add).then_inc(e8, 1)
+
+    e_sl = [ev() for _ in range(H)]
+    if is_rank:
+        for j in range(NCH):
+            V.wait_ge(e_ld[j], 16)
+            Sc.wait_ge(e_ld[j], 16)
+            for hh in (1, 2, 3, 0):
+                out = T.slb[:, hh * SL + j * BCH * W:hh * SL + (j + 1) * BCH * W]
+                in_ = T.cbuf[:, BCH * j:BCH * (j + 1), W * hh:W * (hh + 1)]
+                if hh % 2 == 1:
+                    V.tensor_copy(out, in_).then_inc(e_sl[hh], 1)
+                else:
+                    Sc.activation(out, in_, COPY).then_inc(e_sl[hh], 1)
+        for hh in range(1, H):
+            w = workers[hh]
+            g.wait_ge(e_sl[hh], NCH)
+            rid, pid = topo.addr(w, core)
+            m = topo.mask(core, w)
+            g.remote_dma(T.slb[:, hh * SL:(hh + 1) * SL], T.slb[:, hh * SL:(hh + 1) * SL], T.sem.winS, T.sem.lsem,
+                         pid, rid, m)
+            lsent += len(bits(m))
+        V.wait_ge(e_sl[0], NCH)
+        Sc.wait_ge(e_sl[0], NCH)
+    else:
+        n = len(bits(topo.mask(workers[0], core)))
+        V.wait_ge(T.sem.winS, n)
+        Sc.wait_ge(T.sem.winS, n)
+    V.wait_ge(e8, 2)
+    Sc.wait_ge(e8, 2)
+
+    win = T.slb[:, h * SL:(h + 1) * SL]
+    e_own = ev()
+    turn = 0
+    for call in calls_of(s, core, T, topo):
+        e_g = ev()
+        trs = []
+        for d, m, n in call:
+            out = T.sendbuf[:, d * SLOT:(d + 1) * SLOT]
+            src = win.indirect(T.offS[:, d * 8:(d + 1) * 8])
+            if turn % 2 == 0:
+                V.tensor_copy(out, src).then_inc(e_g, 1)
+            else:
+                Sc.activation(out, src, COPY).then_inc(e_g, 1)
+            turn += 1
+            rid, pid = topo.addr(T.cores[d], core)
+            at = (s * H + h) * SLOT
+            trs.append(RemoteDMATransfer(dst_ids=[DstId(rid=rid, pnc=pid)], dma_engine_mask=m, remote_sem=T.sem.arr,
+                                         srcs=[out], dsts=[T.land[:, at:at + SLOT]], alu_op=0))
+            lsent += n
+        g.wait_ge(e_g, len(call))
+        g.remote_dma_fused(trs, local_sem=T.sem.lsem)
+    if not is_rank:
+        g.wait_ge(T.sem.lsem, lsent)
+        return
+
+    at = (s * H) * SLOT
+    Sc.activation(T.land[:, at:at + SLOT], win.indirect(T.offS[:, s * 8:(s + 1) * 8]), COPY).then_inc(e_own, 1)
+
+    b1, b2, b3, b4, b5, b6, b7 = [ev() for _ in range(7)]
+    V.tensor_copy(T.colf[P, 0:1], T.src4[P, CAPP * s:CAPP * s + 1]).then_inc(b1, 1)
+    V.wait_ge(b1, 1)
+    V.wait_ge(e_cb, 3)
+    V.tensor_scalar(T.Dg8[P, :], T.I8[P, :], T.colf[P, 0:1], None, A.mult).then_inc(b2, 1)
+    Te.wait_ge(e_cb, 3)
+    Te.matmul(T.ps4[:, 0:128], T.Irep[P, :], T.RcB[P, :], True, False)
+    Te.wait_ge(b2, 1)
+    Te.matmul(T.ps3[P, 0:128], T.ones[P, 0:16], T.Dg8[P, :], True, True).then_inc(b3, 1)
+    Te.matmul(T.ps4[:, 0:128], T.c512[P, :], T.Dg8[P, :], False, False)
+    V.wait_ge(b3, 1)
+    V.tensor_scalar(T.Eq[P, :], T.ps3[P, 0:128], T.colf[P, 0:1], None, A.is_equal).then_inc(b4, 1)
+    V.wait_ge(b4, 1)
+    V.tensor_tensor(T.EqU[P, :], T.Eq[P, :], T.U8[P, :], A.mult).then_inc(b5, 1)
+    Te.wait_ge(b5, 1)
+    Te.matmul(T.ps4[:, 0:128], T.c32[P, :], T.EqU[P, :], False, True).then_inc(b6, 1)
+    V.wait_ge(b6, 1)
+    V.tensor_copy(T.offR[:, :], T.ps4[:, 0:128]).then_inc(b7, 1)
+
+    total = 0
+    for r, rc in enumerate(T.cores):
+        for w in chip_workers(rc, T, topo):
+            for call in calls_of(r, w, T, topo):
+                for d, m, n in call:
+                    if d == s:
+                        total += n
+    for q in (V, Sc):
+        q.wait_ge(T.sem.arr, total)
+        q.wait_ge(e_own, 1)
+        q.wait_ge(b7, 1)
+    e_f = [ev() for _ in range(4)]
+    e_st = ev()
+    QW = B * S // 4
+    for j in range(4):
+        out = T.ybuf[:, QW * j:QW * (j + 1)]
+        src = T.land[:, :].indirect(T.offR[:, 32 * j:32 * (j + 1)])
+        if j % 2 == 0:
+            V.tensor_copy(out, src).then_inc(e_f[j], 1)
+        else:
+            Sc.activation(out, src, COPY).then_inc(e_f[j], 1)
+    for j in (0, 2):
+        Sy.wait_ge(e_f[j], 1)
+        Sy.dma_start(T.y[:, QW * j:QW * (j + 1)], T.ybuf[:, QW * j:QW * (j + 1)]).then_inc(e_st, 16)
+    for j in (1, 3):
+        Sc.wait_ge(e_f[j], 1)
+        Sc.dma_start(T.y[:, QW * j:QW * (j + 1)], T.ybuf[:, QW * j:QW * (j + 1)]).then_inc(e_st, 16)
+    g.wait_ge(T.sem.lsem, lsent)
+    g.wait_ge(e_st, 64)

@@ -70,26 +70,21 @@ def common_mask(topo, src, dsts):
 def chip_workers(rc, T, topo):
     same = [c for c in range(NCORES) if topo.host(c) == topo.host(rc) and topo.chip(c) == topo.chip(rc)]
     ok = [c for c in same if c != rc and all(topo.may_write(c, d) for d in T.cores)]
+    ok = [c for c in ok if topo.die(c) != topo.die(rc)] + [c for c in ok if topo.die(c) == topo.die(rc)]
     return [rc] + ok[:H - 1]
 
 
 def calls_of(s, w, T, topo):
     u0 = s // 2
     units = [(u0 + 1 + t) % (N // 2) for t in range(N // 2)]
+    eng = bits(common_mask(topo, w, [c for c in T.cores if c != w]))
+    half = len(eng) // 2
     calls = []
-    for c in range(3):
-        ds = []
-        for u in units[2 * c:2 * c + 2]:
-            ds += [2 * u, 2 * u + 1]
-        ds = [d for d in ds if T.cores[d] != w]
-        eng = bits(common_mask(topo, w, [T.cores[d] for d in ds]))
-        q = len(eng) // 4
-        sizes = [q] * 4 if len(ds) == 4 else [2 * q, q, q]
-        call, at = [], 0
-        for d, n in zip(ds, sizes):
-            call.append((d, to_mask(eng[at:at + n]), n))
-            at += n
-        calls.append(call)
+    for c, u in enumerate(units):
+        ds = [d for d in (2 * u, 2 * u + 1) if T.cores[d] != w]
+        mine = eng[:half] if c % 2 == 0 else eng[half:]
+        n = len(mine) // len(ds)
+        calls.append([(d, to_mask(mine[i * n:(i + 1) * n]), n) for i, d in enumerate(ds)])
     return calls
 
 
@@ -274,18 +269,15 @@ def rank_program(g, core, T, topo):
     e_f = [ev() for _ in range(4)]
     e_st = ev()
     QW = B * S // 4
+    HW = QW // 2
     for j in range(4):
-        out = T.ybuf[:, QW * j:QW * (j + 1)]
-        src = T.land[:, :].indirect(T.offR[:, 32 * j:32 * (j + 1)])
-        if j % 2 == 0:
-            V.tensor_copy(out, src).then_inc(e_f[j], 1)
-        else:
-            Sc.activation(out, src, COPY).then_inc(e_f[j], 1)
-    for j in (0, 2):
-        Sy.wait_ge(e_f[j], 1)
+        a = QW * j
+        V.tensor_copy(T.ybuf[:, a:a + HW],
+                      T.land[:, :].indirect(T.offR[:, 32 * j:32 * j + 16])).then_inc(e_f[j], 1)
+        Sc.activation(T.ybuf[:, a + HW:a + QW],
+                      T.land[:, :].indirect(T.offR[:, 32 * j + 16:32 * j + 32]), COPY).then_inc(e_f[j], 1)
+    for j in range(4):
+        Sy.wait_ge(e_f[j], 2)
         Sy.dma_start(T.y[:, QW * j:QW * (j + 1)], T.ybuf[:, QW * j:QW * (j + 1)]).then_inc(e_st, 16)
-    for j in (1, 3):
-        Sc.wait_ge(e_f[j], 1)
-        Sc.dma_start(T.y[:, QW * j:QW * (j + 1)], T.ybuf[:, QW * j:QW * (j + 1)]).then_inc(e_st, 16)
     g.wait_ge(T.sem.lsem, lsent)
     g.wait_ge(e_st, 64)

from concourse.bass import DstId, RemoteDMATransfer
from concourse.mybir import AluOpType, ActivationFunctionType

N, B, S, CAPP = 12, 16, 128, 4
H = 4
W = S // H
SLOT = CAPP * W
SL = B * W
NCH = 4
BCH = B // NCH
NCORES = 256

SCRATCH = {
    "par": ("sbuf", [128, N], "int32"),
    "cbuf": ("sbuf", [128, B, S], "float32"),
    "slb": ("sbuf", [128, H * SL], "float32"),
    "sendbuf": ("sbuf", [128, N * SLOT], "float32"),
    "land": ("sbuf", [128, N * H * SLOT], "float32"),
    "ybuf": ("sbuf", [128, B * S], "float32"),
    "offS": ("sbuf", [128, N * CAPP * 2], "uint16"),
    "offR": ("sbuf", [128, B * 8], "uint16"),
    "ones": ("sbuf", [128, 128], "float32"),
    "c32": ("sbuf", [128, 128], "float32"),
    "c512": ("sbuf", [128, 128], "float32"),
    "U": ("sbuf", [128, 16], "float32"),
    "Irep": ("sbuf", [128, 128], "float32"),
    "Kc": ("sbuf", [128, 48], "float32"),
    "RcA": ("sbuf", [128, 48], "float32"),
    "U8": ("sbuf", [128, 128], "float32"),
    "I8": ("sbuf", [128, 128], "float32"),
    "RcB": ("sbuf", [128, 128], "float32"),
    "a4": ("sbuf", [128, 48], "int32"),
    "src4": ("sbuf", [128, 48], "int32"),
    "b4": ("sbuf", [128, 48], "int32"),
    "M4": ("sbuf", [128, 48], "float32"),
    "Mb4": ("sbuf", [128, 48], "float32"),
    "E4": ("sbuf", [128, 48], "float32"),
    "V4": ("sbuf", [128, 48], "float32"),
    "colf": ("sbuf", [128, 4], "float32"),
    "Dg8": ("sbuf", [128, 128], "float32"),
    "Eq": ("sbuf", [128, 128], "float32"),
    "EqU": ("sbuf", [128, 128], "float32"),
    "ps1": ("psum", [128, 512], "float32"),
    "ps2": ("psum", [128, 512], "float32"),
    "ps3": ("psum", [128, 512], "float32"),
    "ps4": ("psum", [128, 512], "float32"),
}
NEV = 48
SEMAPHORES = ["parS", "winS", "arr", "lsem"] + ["e%d" % i for i in range(NEV)]


def bits(mask):
    return [e for e in range(16) if (mask >> e) & 1]


def to_mask(engines):
    m = 0
    for e in engines:
        m |= 1 << e
    return m


def common_mask(topo, src, dsts):
    m = topo.mask(src, dsts[0])
    for d in dsts[1:]:
        m &= topo.mask(src, d)
    return m


def chip_workers(rc, T, topo):
    same = [c for c in range(NCORES) if topo.host(c) == topo.host(rc) and topo.chip(c) == topo.chip(rc)]
    ok = [c for c in same if c != rc and all(topo.may_write(c, d) for d in T.cores)]
    ok = [c for c in ok if topo.die(c) != topo.die(rc)] + [c for c in ok if topo.die(c) == topo.die(rc)]
    return [rc] + ok[:H - 1]


def calls_of(s, w, T, topo):
    u0 = s // 2
    units = [(u0 + 1 + t) % (N // 2) for t in range(N // 2)]
    eng = bits(common_mask(topo, w, [c for c in T.cores if c != w]))
    half = len(eng) // 2
    calls = []
    for c, u in enumerate(units):
        ds = [d for d in (2 * u, 2 * u + 1) if T.cores[d] != w]
        mine = eng[:half] if c % 2 == 0 else eng[half:]
        n = len(mine) // len(ds)
        calls.append([(d, to_mask(mine[i * n:(i + 1) * n]), n) for i, d in enumerate(ds)])
    return calls


def rank_program(g, core, T, topo):
    V, Sc, Te, Sy = g.vector, g.scalar, g.tensor, g.sync
    A = AluOpType
    COPY = ActivationFunctionType.Copy
    s, h, workers = None, None, None
    for r, rc in enumerate(T.cores):
        ws = chip_workers(rc, T, topo)
        if core in ws:
            s, h, workers = r, ws.index(core), ws
    if s is None:
        return
    is_rank = h == 0
    nev = [0]

    def ev():
        nev[0] += 1
        return T.sem["e%d" % (nev[0] - 1)]

    lsent = 0
    P = slice(0, 16)

    e_pm, e_parL = ev(), ev()
    if is_rank:
        V.memset(T.par[:, :], 0).then_inc(e_pm, 1)
    e_ones, n_ones = ev(), 2
    V.memset(T.ones[P, :], 1.0).then_inc(e_ones, 1)
    V.memset(T.c32[P, :], float(W)).then_inc(e_ones, 1)
    if is_rank:
        V.memset(T.c512[P, :], float(H * SLOT)).then_inc(e_ones, 1)
        n_ones = 3

    e_ld = [ev() for _ in range(NCH)]
    if is_rank:
        Sy.wait_ge(e_pm, 1)
        Sy.dma_start(T.par[P, :], T.parent[:, :]).then_inc(e_parL, 16)
        for j in range(NCH):
            q = Sc if j % 2 == 0 else Sy
            q.dma_start(T.cbuf[:, BCH * j:BCH * (j + 1), :], T.c[:, BCH * S * j:BCH * S * (j + 1)]).then_inc(e_ld[j], 16)

    e_c = ev()
    g.wait_ge(e_ones, n_ones)
    g.affine_select(T.U[P, 0:16], T.ones[P, 0:16], [[1, 16]], A.is_gt, 0.0, 0, -1).then_inc(e_c, 1)
    g.affine_select(T.Irep[P, :], T.ones[P, :], [[0, 8], [1, 16]], A.is_equal, 0.0, 0, -1).then_inc(e_c, 1)
    g.iota(T.Kc[P, :], [[0, N], [1, CAPP]], 0, 0, allow_small_or_imprecise_dtypes=True).then_inc(e_c, 1)
    g.iota(T.RcA[P, :], [[0, 48]], 0, 1, allow_small_or_imprecise_dtypes=True).then_inc(e_c, 1)

    e_cb = ev()
    if is_rank:
        g.wait_ge(e_parL, 16)
        m = common_mask(topo, core, workers[1:])
        ids = []
        for w in workers[1:]:
            rid, pid = topo.addr(w, core)
            ids.append(DstId(rid=rid, pnc=pid))
        g.remote_dma_fused([RemoteDMATransfer(dst_ids=ids, dma_engine_mask=m, remote_sem=T.sem.parS,
                                              srcs=[T.par[:, :]], dsts=[T.par[:, :] for _ in ids], alu_op=0)],
                           local_sem=T.sem.lsem)
        lsent += len(bits(m))
        V.wait_ge(e_parL, 16)
        g.affine_select(T.U8[P, :], T.ones[P, :], [[1, 16], [0, 8]], A.is_gt, 0.0, 0, -1).then_inc(e_cb, 1)
        g.affine_select(T.I8[P, :], T.ones[P, :], [[1, 16], [0, 8]], A.is_equal, 0.0, 0, -1).then_inc(e_cb, 1)
        g.iota(T.RcB[P, :], [[0, 16], [SLOT, H], [16, 2]], 0, 1, allow_small_or_imprecise_dtypes=True).then_inc(e_cb, 1)
    else:
        V.wait_ge(T.sem.parS, len(bits(common_mask(topo, workers[0], workers[1:]))))

    e1, e2, e3, e4, e5, e6, e7, e8 = [ev() for _ in range(8)]
    Te.wait_ge(e_ones, n_ones)
    Te.wait_ge(e_c, 4)
    Te.matmul(T.ps2[:, 0:48], T.Irep[P, :], T.RcA[P, :], True, False)
    for k in range(CAPP):
        V.tensor_copy(T.a4[P, k:48:CAPP], T.par[P, :]).then_inc(e1, 1)
    V.wait_ge(e1, CAPP)
    V.tensor_scalar(T.src4[P, :], T.a4[P, :], 4, None, A.arith_shift_right).then_inc(e2, 1)
    V.tensor_scalar(T.b4[P, :], T.a4[P, :], 15, None, A.bitwise_and).then_inc(e2, 1)
    V.wait_ge(e2, 2)
    V.tensor_scalar(T.M4[P, :], T.src4[P, :], float(s), None, A.is_equal).then_inc(e3, 1)
    V.wait_ge(e3, 1)
    Te.wait_ge(e3, 1)
    Te.matmul(T.ps1[P, 0:48], T.U[P, 0:16], T.M4[P, :], True, True).then_inc(e4, 1)
    V.tensor_tensor(T.Mb4[P, :], T.M4[P, :], T.b4[P, :], A.mult).then_inc(e5, 1)
    V.wait_ge(e_c, 4)
    V.wait_ge(e4, 1)
    V.tensor_tensor(T.E4[P, :], T.ps1[P, 0:48], T.Kc[P, :], A.is_equal).then_inc(e5, 1)
    V.wait_ge(e5, 2)
    V.tensor_tensor(T.V4[P, :], T.E4[P, :], T.Mb4[P, :], A.mult).then_inc(e6, 1)
    Te.wait_ge(e6, 1)
    Te.matmul(T.ps2[:, 0:48], T.c32[P, :], T.V4[P, :], False, True).then_inc(e7, 1)
    V.wait_ge(e7, 1)
    for xh in range(2):
        V.tensor_scalar(T.offS[:, xh:96:2], T.ps2[:, 0:48], float(16 * xh), None, A.add).then_inc(e8, 1)

    e_sl = [ev() for _ in range(H)]
    if is_rank:
        for j in range(NCH):
            V.wait_ge(e_ld[j], 16)
            Sc.wait_ge(e_ld[j], 16)
            for hh in (1, 2, 3, 0):
                out = T.slb[:, hh * SL + j * BCH * W:hh * SL + (j + 1) * BCH * W]
                in_ = T.cbuf[:, BCH * j:BCH * (j + 1), W * hh:W * (hh + 1)]
                if hh % 2 == 1:
                    V.tensor_copy(out, in_).then_inc(e_sl[hh], 1)
                else:
                    Sc.activation(out, in_, COPY).then_inc(e_sl[hh], 1)
        for hh in range(1, H):
            w = workers[hh]
            g.wait_ge(e_sl[hh], NCH)
            rid, pid = topo.addr(w, core)
            m = topo.mask(core, w)
            g.remote_dma(T.slb[:, hh * SL:(hh + 1) * SL], T.slb[:, hh * SL:(hh + 1) * SL], T.sem.winS, T.sem.lsem,
                         pid, rid, m)
            lsent += len(bits(m))
        V.wait_ge(e_sl[0], NCH)
        Sc.wait_ge(e_sl[0], NCH)
    else:
        n = len(bits(topo.mask(workers[0], core)))
        V.wait_ge(T.sem.winS, n)
        Sc.wait_ge(T.sem.winS, n)
    V.wait_ge(e8, 2)
    Sc.wait_ge(e8, 2)

    win = T.slb[:, h * SL:(h + 1) * SL]
    e_own = ev()
    turn = 0
    for call in calls_of(s, core, T, topo):
        e_g = ev()
        trs = []
        for d, m, n in call:
            out = T.sendbuf[:, d * SLOT:(d + 1) * SLOT]
            src = win.indirect(T.offS[:, d * 8:(d + 1) * 8])
            if turn % 2 == 0:
                V.tensor_copy(out, src).then_inc(e_g, 1)
            else:
                Sc.activation(out, src, COPY).then_inc(e_g, 1)
            turn += 1
            rid, pid = topo.addr(T.cores[d], core)
            at = (s * H + h) * SLOT
            trs.append(RemoteDMATransfer(dst_ids=[DstId(rid=rid, pnc=pid)], dma_engine_mask=m, remote_sem=T.sem.arr,
                                         srcs=[out], dsts=[T.land[:, at:at + SLOT]], alu_op=0))
            lsent += n
        g.wait_ge(e_g, len(call))
        g.remote_dma_fused(trs, local_sem=T.sem.lsem)
    if not is_rank:
        g.wait_ge(T.sem.lsem, lsent)
        return

    at = (s * H) * SLOT
    Sc.activation(T.land[:, at:at + SLOT], win.indirect(T.offS[:, s * 8:(s + 1) * 8]), COPY).then_inc(e_own, 1)

    b1, b2, b3, b4, b5, b6, b7 = [ev() for _ in range(7)]
    V.tensor_copy(T.colf[P, 0:1], T.src4[P, CAPP * s:CAPP * s + 1]).then_inc(b1, 1)
    V.wait_ge(b1, 1)
    V.wait_ge(e_cb, 3)
    V.tensor_scalar(T.Dg8[P, :], T.I8[P, :], T.colf[P, 0:1], None, A.mult).then_inc(b2, 1)
    Te.wait_ge(e_cb, 3)
    Te.matmul(T.ps4[:, 0:128], T.Irep[P, :], T.RcB[P, :], True, False)
    Te.wait_ge(b2, 1)
    Te.matmul(T.ps3[P, 0:128], T.ones[P, 0:16], T.Dg8[P, :], True, True).then_inc(b3, 1)
    Te.matmul(T.ps4[:, 0:128], T.c512[P, :], T.Dg8[P, :], False, False)
    V.wait_ge(b3, 1)
    V.tensor_scalar(T.Eq[P, :], T.ps3[P, 0:128], T.colf[P, 0:1], None, A.is_equal).then_inc(b4, 1)
    V.wait_ge(b4, 1)
    V.tensor_tensor(T.EqU[P, :], T.Eq[P, :], T.U8[P, :], A.mult).then_inc(b5, 1)
    Te.wait_ge(b5, 1)
    Te.matmul(T.ps4[:, 0:128], T.c32[P, :], T.EqU[P, :], False, True).then_inc(b6, 1)
    V.wait_ge(b6, 1)
    V.tensor_copy(T.offR[:, :], T.ps4[:, 0:128]).then_inc(b7, 1)

    total = 0
    for r, rc in enumerate(T.cores):
        for w in chip_workers(rc, T, topo):
            for call in calls_of(r, w, T, topo):
                for d, m, n in call:
                    if d == s:
                        total += n
    for q in (V, Sc):
        q.wait_ge(T.sem.arr, total)
        q.wait_ge(e_own, 1)
        q.wait_ge(b7, 1)
    e_f = [ev() for _ in range(4)]
    e_st = ev()
    QW = B * S // 4
    HW = QW // 2
    for j in range(4):
        a = QW * j
        V.tensor_copy(T.ybuf[:, a:a + HW],
                      T.land[:, :].indirect(T.offR[:, 32 * j:32 * j + 16])).then_inc(e_f[j], 1)
        Sc.activation(T.ybuf[:, a + HW:a + QW],
                      T.land[:, :].indirect(T.offR[:, 32 * j + 16:32 * j + 32]), COPY).then_inc(e_f[j], 1)
    for j in range(4):
        Sy.wait_ge(e_f[j], 2)
        Sy.dma_start(T.y[:, QW * j:QW * (j + 1)], T.ybuf[:, QW * j:QW * (j + 1)]).then_inc(e_st, 16)
    g.wait_ge(T.sem.lsem, lsent)
    g.wait_ge(e_st, 64)
